import numpy as np
import ml_dtypes


def mxq(x, axis, fmt="e4m3"):
    dtype, down = {"e4m3": (ml_dtypes.float8_e4m3fn, 7), "e5m2": (ml_dtypes.float8_e5m2, 14)}[fmt]
    v = np.moveaxis(np.asarray(x, np.float32).astype(ml_dtypes.bfloat16).astype(np.float64), axis, -1)
    blocks = v.reshape(v.shape[:-1] + (-1, 32))
    amax = np.abs(blocks).max(-1, keepdims=True)
    byte = np.maximum(np.where(amax > 0, np.frexp(amax)[1] - 1 + 127, 0) - down, 1)
    scale = np.exp2(byte - 127.0)
    codes = (blocks / scale).astype(np.float32).astype(dtype).astype(np.float64)
    return np.moveaxis((codes * scale).reshape(v.shape), -1, axis)


WIDE = False


def mx_kscale(k):
    if not WIDE:
        return np.ones(k)
    levels = np.array([10, -10, 5, -5, 0])
    if k % 512:
        return np.exp2(np.random.permutation(np.resize(levels, k // 32))).repeat(32)
    a = np.empty((k // 512, 16))
    for p in range(k // 512):
        a[p, :8] = np.random.permutation(np.resize(levels, 8))
        for g in range(8):
            far = levels[np.abs(levels - a[p, g]) >= 10]
            a[p, g + 8] = far[np.random.randint(len(far))]
    return np.exp2(a.ravel()).repeat(32)


BF16 = ml_dtypes.bfloat16


def bf(x):
    return np.asarray(x, np.float32).astype(BF16)


def f64(x):
    return np.asarray(x).astype(np.float64)


E2M1 = np.array([0.0, 0.5, 1.0, 1.5, 2.0, 3.0, 4.0, 6.0, -0.0, -0.5, -1.0, -1.5, -2.0, -3.0, -4.0, -6.0])


def pack_weight(w, fmt):
    k, n = w.shape
    w = f64(bf(w)).reshape(k // 32, 32, n)
    amax = np.abs(w).max(1)
    if fmt == "e4m3":
        byte = np.frexp(amax)[1] - 1 + 127 - 7
    else:
        mant, ex = np.frexp(amax / 6.0)
        byte = np.where(mant > 0.5, ex, ex - 1) + 127
    byte = np.clip(np.where(amax > 0, byte, 1), 1, 254)
    scaled = (w * np.exp2(127.0 - byte)[:, None, :]).reshape(k, n).astype(np.float32)
    by_word = np.ascontiguousarray(scaled.reshape(k // 512, 128, 4, n).transpose(0, 1, 3, 2))
    if fmt == "e4m3":
        words = by_word.astype(ml_dtypes.float8_e4m3fn).view(np.uint8)
    else:
        c = by_word.astype(ml_dtypes.float4_e2m1fn).view(np.uint8) & 0xF
        words = c[..., 0::2] | (c[..., 1::2] << 4)
    return np.ascontiguousarray(words), np.ascontiguousarray(byte.astype(np.uint8).reshape(k // 512, 16, n))


def unpack_weight(words, scales, fmt):
    g, p, n, _ = words.shape
    if fmt == "e4m3":
        vals = np.ascontiguousarray(words).view(ml_dtypes.float8_e4m3fn).astype(np.float64)
    else:
        nib = np.empty((g, p, n, 4), np.uint8)
        nib[..., 0::2] = words & 0xF
        nib[..., 1::2] = words >> 4
        vals = E2M1[nib]
    vals = vals * np.repeat(np.exp2(scales.astype(np.float64) - 127.0), 8, axis=1)[..., None]
    return vals.transpose(0, 1, 3, 2).reshape(g * 512, n)
def pack4(w):
    words, scales = pack_weight(w, "e2m1")
    return words.reshape(words.shape[0], 128, -1), scales


def unpack4(words, scales):
    return unpack_weight(words.reshape(words.shape[0], 128, -1, 2), scales, "e2m1")


def planes(Y):
    n, m = Y.shape
    b = f64(bf(Y)).reshape(n // 32, 32, m)
    amax = np.abs(b).max(1)
    byte = np.clip(np.where(amax > 0, np.frexp(amax)[1] - 1 + 127 - 7, 1), 1, 254)
    codes = (b * np.exp2(127.0 - byte)[:, None, :]).reshape(n, m).astype(np.float32).astype(ml_dtypes.float8_e4m3fn).view(np.uint8)
    words = codes.reshape(n // 512, 128, 4, m).transpose(0, 1, 3, 2)
    return np.ascontiguousarray(words), np.ascontiguousarray(byte.astype(np.uint8).reshape(n // 512, 16, m))


M, K, F, N = 1024, 1536, 1024, 1536
SOFT = 0.4
UNIT = 4.0

def softened_coulomb(sites, points):
    d2 = sum((sites[:, i][:, None] - points[:, i][None, :]) ** 2 for i in range(3))
    return 1.0 / np.sqrt(d2 + SOFT ** 2)

def setup_inputs():
    s, t = mx_kscale(K), mx_kscale(F)
    sites, points = np.random.randn(K, 3), np.random.randn(F, 3)
    charges = np.random.randn(M, K)
    charges = charges - charges.mean(axis=1, keepdims=True)
    x_words, x_scales = pack_weight(charges.T * s[:, None], "e4m3")
    kernel = UNIT / np.sqrt(K) * softened_coulomb(sites, points)
    c_words, c_scales = pack4(kernel / s[:, None] * t[None, :])
    v = bf(-points[:, 2] * t)
    field = bf(0.6 * np.random.randn(M))
    width = np.exp(0.8 * np.random.randn(N))
    r = bf(np.random.randn(F, N) / np.sqrt(F) * width[None, :] / t[:, None])
    prev = bf(np.random.randn(M, N) * width[None, :])
    eta = bf(np.random.uniform(0.3, 0.7, N))
    return dict(x_words=x_words, x_scales=x_scales, c_words=c_words, c_scales=c_scales,
                v=v, field=field, r=r, prev=prev, eta=eta)

def reference(x_words, x_scales, c_words, c_scales, v, field, r, prev, eta):
    A = unpack_weight(x_words, x_scales, "e4m3")
    C = unpack4(c_words, c_scales)
    u = (A.T @ C) + f64(field)[:, None] * f64(v)[None, :]
    z = mxq(u, 1, "e4m3") @ mxq(f64(r), 0, "e4m3")
    y = f64(eta)[None, :] * z + (1.0 - f64(eta))[None, :] * f64(prev)
    Y = y.T
    words, scales = planes(Y)
    return y, words, scales

@@ -1,0 +1,423 @@
+from contextlib import ExitStack
+
+import concourse.mybir as mybir
+from concourse.masks import make_identity
+
+M, K, F, N = 1024, 1536, 1024, 1536
+FLOPS = 2 * M * K * F + 2 * M * F * N
+
+F32 = mybir.dt.float32
+BF16 = mybir.dt.bfloat16
+I32 = mybir.dt.int32
+U32 = mybir.dt.uint32
+U8 = mybir.dt.uint8
+FP8X4 = mybir.dt.float8_e4m3fn_x4
+FP4X4 = mybir.dt.float4_e2m1fn_x4
+ALU = mybir.AluOpType
+ACT = mybir.ActivationFunctionType
+
+P = 128
+PACK = 4
+PASS = P * PACK
+KG = K // PASS
+FG = F // PASS
+NG = N // PASS
+HALF = 512
+MT = M // P
+PAIRS = MT // 2
+UNITS = [(0, 0, 512), (0, 512, 512), (1, 0, 512), (1, 512, 512), (2, 0, 512), (2, 512, 256), (2, 768, 256)]
+R_ENGINE = {(0, 0): "S", (0, 1): "G", (1, 0): "S", (1, 1): "G", (2, 0): "G", (2, 1): "S"}
+Y_ENGINE = ["G", "G", "G", "G", "G", "G", "V"]
+BANKS = 8
+
+
+def tile_coulomb_response_mixing_h2_kernel(
+    tc, x_words, x_scales, c_words, c_scales, v, field, r, prev, eta, out_0, out_1, out_2
+):
+    nc = tc.nc
+    with ExitStack() as ctx:
+        keep = ctx.enter_context(tc.tile_pool(name="keep", bufs=1))
+        stage = ctx.enter_context(tc.tile_pool(name="stage", bufs=3))
+        psum = ctx.enter_context(tc.psum_pool(name="psum", bufs=1))
+        ctx.enter_context(tc.manual_schedule())
+
+        banks_taken = []
+
+        def next_bank(dtype=F32):
+            i = len(banks_taken)
+            banks_taken.append(i)
+            width = 512 if dtype == F32 else 1024
+            return psum.tile([P, width], dtype, name="bank%d" % i, tag="bank%d" % (i % BANKS))
+
+        x_codes = keep.tile([P, 2, KG, HALF], U32, name="x_codes", align_bytes=64)
+        x_sc = keep.tile([P, KG, M], U8, name="x_sc", align_bytes=64)
+        c_codes = keep.tile([P, KG, 2 * F], U8, name="c_codes", align_bytes=64)
+        c_sc = keep.tile([P, KG, F], U8, name="c_sc", align_bytes=64)
+        r_raw = keep.tile([P, NG, FG, PACK, PASS], BF16, name="r_raw", align_bytes=64)
+        r_codes = keep.tile([P, NG, FG, PASS], U32, name="r_codes", align_bytes=64)
+        r_sc = keep.tile([P, NG, FG, PASS], U8, name="r_sc", align_bytes=64)
+        prev_sb = keep.tile([P, NG, MT, PASS], BF16, name="prev_sb", align_bytes=64)
+        u_codes = keep.tile([P, FG, M], U32, name="u_codes", align_bytes=64)
+        u_sc = keep.tile([P, FG, M], U8, name="u_sc", align_bytes=64)
+        y_codes = keep.tile([P, NG, M], U32, name="y_codes", align_bytes=64)
+        y_sc = keep.tile([P, NG, M], U8, name="y_sc", align_bytes=64)
+        ident_f = keep.tile([P, P], F32, name="ident_f", align_bytes=64)
+        ident_b = keep.tile([P, P], BF16, name="ident_b", align_bytes=64)
+        v_cols = keep.tile([P, FG, PACK], BF16, name="v_cols", align_bytes=64)
+        v_rows = keep.tile([P, F], BF16, name="v_rows", align_bytes=64)
+        field_rows = keep.tile([P, P], BF16, name="field_rows", align_bytes=64)
+        field_cols = keep.tile([P, MT], F32, name="field_cols", align_bytes=64)
+        eta_b = keep.tile([P, NG, PACK], BF16, name="eta_b", align_bytes=64)
+        eta_f = keep.tile([P, NG * PACK], F32, name="eta_f", align_bytes=64)
+        rest_f = keep.tile([P, NG * PACK], F32, name="rest_f", align_bytes=64)
+
+        x_view = x_words.rearrange("g p m t -> p g (m t)").bitcast(I32)
+        c_view = c_words.rearrange("g p b -> p g b").bitcast(I32)
+
+        def load_x(h, g0, g1):
+            nc.sync.dma_start(
+                out=x_codes[:, h, g0:g1, :].bitcast(I32), in_=x_view[:, g0:g1, h * HALF : (h + 1) * HALF]
+            )
+
+        def load_c(g0, g1):
+            nc.sync.dma_start(out=c_codes[:, g0:g1, :].bitcast(I32), in_=c_view[:, g0:g1, :])
+
+        def load_scales(engine, tile, src, q):
+            engine.dma_start(
+                out=tile[32 * q : 32 * q + 4, :, :].bitcast(I32),
+                in_=src.rearrange("g q n -> q g n")[4 * q : 4 * q + 4].bitcast(I32),
+            )
+
+        def load_r(c, g):
+            rows = r[g * PASS : (g + 1) * PASS, c * PASS : (c + 1) * PASS]
+            nc.sync.dma_start(out=r_raw[:, c, g, :, :], in_=rows.rearrange("(p j) n -> p j n", j=PACK))
+
+        def load_prev(c, h):
+            rows = prev[h * HALF : (h + 1) * HALF, c * PASS : (c + 1) * PASS]
+            nc.sync.dma_start(out=prev_sb[:, c, 4 * h : 4 * h + 4, :], in_=rows.rearrange("(a p) n -> p a n", p=P))
+
+        def regroup(engine, dst, src):
+            if engine == "S":
+                nc.scalar.copy(out=dst, in_=src)
+            elif engine == "V":
+                nc.vector.tensor_copy(out=dst, in_=src)
+            else:
+                nc.gpsimd.tensor_scalar(out=dst, in0=src, scalar1=1.0, scalar2=1.0, op0=ALU.mult, op1=ALU.mult)
+
+        u_banks = {}
+        u_rows = {}
+        ut_banks = {}
+        u_grp = {}
+        r_grp = {}
+
+        def first_pass(mt, g, kg):
+            if kg == 0:
+                u_banks[mt, g] = next_bank()
+            col = (mt % 4) * P
+            nc.tensor.matmul_mx(
+                out=u_banks[mt, g][:],
+                lhsT=x_codes[:, mt // 4, kg, col : col + P].bitcast(FP8X4),
+                lhsT_scale=x_sc[:, kg, mt * P : (mt + 1) * P],
+                rhs=c_codes[:, kg, 2 * g * PASS : 2 * (g + 1) * PASS].bitcast(FP4X4),
+                rhs_scale=c_sc[:, kg, g * PASS : (g + 1) * PASS],
+                start=(kg == 0),
+                stop=(kg == KG - 1),
+            )
+
+        def first_product(pair):
+            for mt in (2 * pair, 2 * pair + 1):
+                for g in range(FG):
+                    for kg in range(KG):
+                        first_pass(mt, g, kg)
+
+        def add_external(mt):
+            rows = stage.tile([P, FG, 2, P, 2], BF16, name="u_rows%d" % mt, tag="u_rows", bufs=4, align_bytes=64)
+            u_rows[mt] = rows
+            for g in range(FG):
+                sums = u_banks[mt, g][:].rearrange("m (p w e) -> m w p e", w=2, e=2)
+                for w in range(2):
+                    lo = (2 * g + w) * 2 * P
+                    nc.vector.scalar_tensor_tensor(
+                        out=rows[:, g, w, :, :],
+                        in0=v_rows[:, lo : lo + 2 * P].rearrange("m (p e) -> m p e", e=2),
+                        scalar=field_cols[:, mt : mt + 1],
+                        in1=sums[:, w, :, :],
+                        op0=ALU.mult,
+                        op1=ALU.add,
+                    )
+
+        def turn_u(pair):
+            for mt in (2 * pair, 2 * pair + 1):
+                bank = next_bank()
+                ut_banks[mt] = bank
+                words = u_rows[mt][:].rearrange("m g w p e -> m (g w p e)").bitcast(F32)
+                for a in range(2 * FG):
+                    nc.tensor.transpose(bank[:, a * P : (a + 1) * P], words[:, a * P : (a + 1) * P], ident_f[:])
+
+        def copy_u(pair):
+            h = pair // 2
+            if pair % 2 == 0:
+                u_grp[h] = stage.tile([P, FG, HALF * PACK], BF16, name="u_grp%d" % h, tag="u_grp", bufs=2, align_bytes=64)
+            words = u_grp[h][:].bitcast(F32).rearrange("p g (s m w) -> p s g m w", s=4, w=2)
+            for s in range(2):
+                nc.scalar.copy(
+                    out=words[:, 2 * (pair % 2) + s, :, :, :],
+                    in_=ut_banks[2 * pair + s][:].rearrange("p (g w m) -> p g m w", g=FG, w=2),
+                )
+
+        def quantize_u(h, g):
+            cols = slice(HALF * h, HALF * (h + 1))
+            nc.vector.quantize_mx(
+                out=u_codes[:, g, cols].bitcast(FP8X4), scales=u_sc[:, g, cols], in_=u_grp[h][:, g, :]
+            )
+
+        def group_r(c, g):
+            grp = stage.tile([P, PACK * PASS], BF16, name="r_grp%d%d" % (c, g), tag="r_grp", bufs=5, align_bytes=64)
+            r_grp[c, g] = grp
+            dst = grp[:].rearrange("p (t n j) -> p t n j", t=PACK, j=PACK)
+            src = r_raw[:, c, g, :, :].rearrange("p j (n t) -> p t n j", t=PACK)
+            if R_ENGINE[c, g] == "G":
+                for t in range(PACK):
+                    regroup("G", dst[:, t], src[:, t])
+            else:
+                regroup(R_ENGINE[c, g], dst, src)
+
+        def quantize_r(c, g):
+            nc.vector.quantize_mx(
+                out=r_codes[:, c, g, :].bitcast(FP8X4), scales=r_sc[:, c, g, :], in_=r_grp[c, g][:]
+            )
+
+        prev_banks = {}
+        kept = {}
+        z_banks = {}
+        y_t = {}
+        y_banks = {}
+        y_grp = {}
+
+        def turn_prev(i):
+            c, m0, width = i // 2, (i % 2) * HALF, HALF
+            words = prev_sb[:, c, :, :].bitcast(F32)
+            for w in range(2):
+                bank = next_bank()
+                prev_banks[i, w] = bank
+                for a in range(width // P):
+                    nc.tensor.transpose(bank[:, a * P : (a + 1) * P], words[:, m0 // P + a, w::2], ident_f[:])
+
+        def scale_prev(i):
+            c, width = i // 2, HALF
+            tile = stage.tile([P, PACK, width], F32, name="kept%d" % i, tag="kept", bufs=2, align_bytes=64)
+            kept[i] = tile
+            for t in range(PACK):
+                pairs = prev_banks[i, t // 2][:, 0:width].bitcast(BF16).rearrange("p (m e) -> p e m", e=2)
+                nc.scalar.activation(
+                    out=tile[:, t, :],
+                    in_=pairs[:, t % 2, :],
+                    func=ACT.Copy,
+                    scale=rest_f[:, PACK * c + t : PACK * c + t + 1],
+                )
+
+        def second_product(i):
+            c, m0, width = UNITS[i]
+            cols = slice(m0, m0 + width)
+            per_bank = HALF // width
+            for t in range(PACK):
+                if t % per_bank == 0:
+                    bank = next_bank()
+                lo = (t % per_bank) * width
+                z_banks[i, t] = bank[:, lo : lo + width]
+                for g in range(FG):
+                    nc.tensor.matmul_mx(
+                        out=z_banks[i, t],
+                        lhsT=r_codes[:, c, g, t * P : (t + 1) * P].bitcast(FP8X4),
+                        lhsT_scale=r_sc[:, c, g, t * P : (t + 1) * P],
+                        rhs=u_codes[:, g, cols].bitcast(FP8X4),
+                        rhs_scale=u_sc[:, g, cols],
+                        start=(g == 0),
+                        stop=(g == FG - 1),
+                    )
+
+        def mix(i, slots):
+            c, m0, width = UNITS[i]
+            if 0 in slots:
+                y_t[i] = stage.tile([P, PACK, width], F32, name="y_t%d" % i, tag="y_t", bufs=3, align_bytes=64)
+            tile = y_t[i]
+            for t in slots:
+                nc.vector.scalar_tensor_tensor(
+                    out=tile[:, t, :],
+                    in0=z_banks[i, t],
+                    scalar=eta_f[:, PACK * c + t : PACK * c + t + 1],
+                    in1=kept[2 * c + m0 // HALF][:, t, m0 % HALF : m0 % HALF + width],
+                    op0=ALU.mult,
+                    op1=ALU.add,
+                )
+
+        def turn_y(i):
+            tiles = range(UNITS[i][2] // P)
+            for a in tiles:
+                y_banks[i, a] = next_bank()
+            for t in range(PACK):
+                for a in tiles:
+                    nc.tensor.transpose(
+                        y_banks[i, a][:, t * P : (t + 1) * P], y_t[i][:, t, a * P : (a + 1) * P], ident_f[:]
+                    )
+
+        def store_y(i, a, engine):
+            c, m0, width = UNITS[i]
+            rows = stage.tile([P, PASS], F32, name="y_rows%d%d" % (i, a), tag="y_rows", bufs=8, align_bytes=64)
+            regroup(
+                engine,
+                rows[:].rearrange("m (p t) -> m p t", t=PACK),
+                y_banks[i, a][:].rearrange("m (t p) -> m p t", t=PACK),
+            )
+            lo = m0 + a * P
+            nc.sync.dma_start(out=out_0[lo : lo + P, c * PASS : (c + 1) * PASS], in_=rows[:])
+
+        def group_y(i):
+            width = UNITS[i][2]
+            grp = stage.tile([P, width * PACK], BF16, name="y_grp%d" % i, tag="y_grp", bufs=2, align_bytes=64)
+            y_grp[i] = grp
+            dst = grp[:].rearrange("p (m t) -> p m t", t=PACK)
+            src = y_t[i][:].rearrange("p t m -> p m t")
+            pieces = 2 if Y_ENGINE[i] == "G" else 1
+            step = width // pieces
+            for k in range(pieces):
+                regroup(Y_ENGINE[i], dst[:, k * step : (k + 1) * step], src[:, k * step : (k + 1) * step])
+
+        def quantize_y(i):
+            c, m0, width = UNITS[i]
+            cols = slice(m0, m0 + width)
+            nc.vector.quantize_mx(out=y_codes[:, c, cols].bitcast(FP8X4), scales=y_sc[:, c, cols], in_=y_grp[i][:])
+
+        def store_planes(i):
+            c, m0, width = UNITS[i]
+            cols = slice(m0, m0 + width)
+            dst = out_1[c].rearrange("p m t -> p (m t)").bitcast(I32)
+            nc.sync.dma_start(out=dst[:, cols], in_=y_codes[:, c, cols].bitcast(I32))
+            if m0 + width == M:
+                for q in range(4):
+                    nc.sync.dma_start(
+                        out=out_2[c, 4 * q : 4 * q + 4, :].bitcast(I32),
+                        in_=y_sc[32 * q : 32 * q + 4, c, :].bitcast(I32),
+                    )
+
+        nc.gpsimd.memset(c_sc[:].bitcast(I32), 0)
+        nc.vector.memset(x_sc[:].bitcast(I32), 0)
+        nc.vector.memset(field_rows[:], 0.0)
+        make_identity(nc, ident_b[:])
+        make_identity(nc, ident_f[:])
+        load_c(0, 1)
+        load_x(0, 0, 1)
+        for q in range(4):
+            load_scales(nc.sync, x_sc, x_scales, q)
+        for q in range(4):
+            load_scales(nc.sync, c_sc, c_scales, q)
+        nc.sync.dma_start(out=v_cols[:], in_=v.rearrange("(g p t) -> p g t", g=FG, t=PACK))
+        nc.sync.dma_start(out=field_rows[0:MT, :], in_=field.rearrange("(a p) -> a p", p=P))
+        load_c(1, KG)
+        load_x(0, 1, KG)
+        load_r(0, 0)
+        load_r(0, 1)
+        load_x(1, 0, KG)
+        load_r(1, 0)
+        load_r(1, 1)
+        nc.sync.dma_start(out=eta_b[:], in_=eta.rearrange("(c p t) -> p c t", c=NG, t=PACK))
+        load_r(2, 0)
+        load_r(2, 1)
+        load_prev(0, 0)
+        load_prev(0, 1)
+        for c in range(1, NG):
+            load_prev(c, 0)
+            load_prev(c, 1)
+
+        for mt in range(2):
+            for g in range(FG):
+                first_pass(mt, g, 0)
+        v_bank = next_bank(BF16)
+        for a in range(FG * PACK):
+            col = v_cols[:].rearrange("p g t -> p (g t)")[:, a : a + 1]
+            nc.tensor.transpose(v_bank[:, a * P : (a + 1) * P], col.to_broadcast([P, P]), ident_b[:])
+        field_bank = next_bank(BF16)
+        nc.tensor.transpose(field_bank[:, 0:P], field_rows[:], ident_b[:])
+        for kg in range(1, KG):
+            for mt in range(2):
+                for g in range(FG):
+                    first_pass(mt, g, kg)
+        nc.scalar.activation(out=field_cols[:], in_=field_bank[:, 0:MT], func=ACT.Copy)
+        nc.vector.tensor_copy(
+            out=v_rows[:].rearrange("m (a p e) -> m a p e", p=P, e=2),
+            in_=v_bank[:].rearrange("m (a e p) -> m a p e", p=P, e=2),
+        )
+
+        add_external(0)
+        add_external(1)
+        first_product(1)
+        group_r(0, 0)
+        group_r(0, 1)
+        turn_u(0)
+        add_external(2)
+        add_external(3)
+        copy_u(0)
+        first_product(2)
+        quantize_r(0, 0)
+        group_r(1, 0)
+        group_r(1, 1)
+        turn_u(1)
+        copy_u(1)
+        add_external(4)
+        add_external(5)
+        first_product(3)
+        quantize_r(0, 1)
+        group_r(2, 0)
+        group_r(2, 1)
+        eta_flat = eta_b[:].rearrange("p c t -> p (c t)")
+        nc.scalar.copy(out=eta_f[:], in_=eta_flat)
+        nc.scalar.activation(out=rest_f[:], in_=eta_flat, func=ACT.Copy, scale=-1.0, bias=1.0)
+        turn_u(2)
+        add_external(6)
+        add_external(7)
+        copy_u(2)
+        turn_prev(0)
+        scale_prev(0)
+        turn_u(3)
+        copy_u(3)
+        quantize_u(0, 0)
+        quantize_u(0, 1)
+        quantize_r(1, 0)
+        quantize_r(1, 1)
+        second_product(0)
+        for i in range(5):
+            mix(i, (0, 1, 2))
+            if i == 0:
+                quantize_u(1, 0)
+            if i in (1, 2):
+                quantize_r(2, i - 1)
+            mix(i, (3,))
+            if i == 0:
+                quantize_u(1, 1)
+            if i > 0:
+                quantize_y(i - 1)
+                store_planes(i - 1)
+            turn_prev(i + 1)
+            turn_y(i)
+            group_y(i)
+            scale_prev(i + 1)
+            second_product(i + 1)
+            for a in range(4):
+                store_y(i, a, "V" if a == 0 else "S")
+        second_product(6)
+        mix(5, range(PACK))
+        quantize_y(4)
+        store_planes(4)
+        turn_y(5)
+        group_y(5)
+        mix(6, range(PACK))
+        turn_y(6)
+        store_y(5, 0, "S")
+        store_y(5, 1, "S")
+        quantize_y(5)
+        store_planes(5)
+        group_y(6)
+        store_y(6, 0, "S")
+        store_y(6, 1, "S")
+        quantize_y(6)
+        store_planes(6)

@@ -26,7 +26,7 @@ HALF = 512
 MT = M // P
 PAIRS = MT // 2
 UNITS = [(0, 0, 512), (0, 512, 512), (1, 0, 512), (1, 512, 512), (2, 0, 512), (2, 512, 256), (2, 768, 256)]
-R_ENGINE = {(0, 0): "S", (0, 1): "G", (1, 0): "S", (1, 1): "G", (2, 0): "G", (2, 1): "S"}
+R_ENGINE = {(0, 0): "S", (0, 1): "G", (1, 0): "S", (1, 1): "G", (2, 0): "S", (2, 1): "G"}
 Y_ENGINE = ["G", "G", "G", "G", "G", "G", "V"]
 BANKS = 8
 
@@ -50,7 +50,7 @@ def tile_coulomb_response_mixing_h2_kernel(
             return psum.tile([P, width], dtype, name="bank%d" % i, tag="bank%d" % (i % BANKS))
 
         x_codes = keep.tile([P, 2, KG, HALF], U32, name="x_codes", align_bytes=64)
-        x_sc = keep.tile([P, KG, M], U8, name="x_sc", align_bytes=64)
+        x_sc = keep.tile([P, 2, KG, HALF], U8, name="x_sc", align_bytes=64)
         c_codes = keep.tile([P, KG, 2 * F], U8, name="c_codes", align_bytes=64)
         c_sc = keep.tile([P, KG, F], U8, name="c_sc", align_bytes=64)
         r_raw = keep.tile([P, NG, FG, PACK, PASS], BF16, name="r_raw", align_bytes=64)
@@ -82,11 +82,12 @@ def tile_coulomb_response_mixing_h2_kernel(
         def load_c(g0, g1):
             nc.sync.dma_start(out=c_codes[:, g0:g1, :].bitcast(I32), in_=c_view[:, g0:g1, :])
 
-        def load_scales(engine, tile, src, q):
-            engine.dma_start(
-                out=tile[32 * q : 32 * q + 4, :, :].bitcast(I32),
-                in_=src.rearrange("g q n -> q g n")[4 * q : 4 * q + 4].bitcast(I32),
-            )
+        def load_scales(tile, src, lo, hi):
+            for j in range(4):
+                nc.sync.dma_start(
+                    out=tile[j:P:32].bitcast(I32),
+                    in_=src.rearrange("g (q j) n -> j q g n", j=4)[j, :, :, lo:hi].bitcast(I32),
+                )
 
         def load_r(c, g):
             rows = r[g * PASS : (g + 1) * PASS, c * PASS : (c + 1) * PASS]
@@ -117,7 +118,7 @@ def tile_coulomb_response_mixing_h2_kernel(
             nc.tensor.matmul_mx(
                 out=u_banks[mt, g][:],
                 lhsT=x_codes[:, mt // 4, kg, col : col + P].bitcast(FP8X4),
-                lhsT_scale=x_sc[:, kg, mt * P : (mt + 1) * P],
+                lhsT_scale=x_sc[:, mt // 4, kg, col : col + P],
                 rhs=c_codes[:, kg, 2 * g * PASS : 2 * (g + 1) * PASS].bitcast(FP4X4),
                 rhs_scale=c_sc[:, kg, g * PASS : (g + 1) * PASS],
                 start=(kg == 0),
@@ -154,25 +155,30 @@ def tile_coulomb_response_mixing_h2_kernel(
                 for a in range(2 * FG):
                     nc.tensor.transpose(bank[:, a * P : (a + 1) * P], words[:, a * P : (a + 1) * P], ident_f[:])
 
-        def copy_u(pair):
+        def copy_u(pair, engines="SS"):
             h = pair // 2
             if pair % 2 == 0:
                 u_grp[h] = stage.tile([P, FG, HALF * PACK], BF16, name="u_grp%d" % h, tag="u_grp", bufs=2, align_bytes=64)
             words = u_grp[h][:].bitcast(F32).rearrange("p g (s m w) -> p s g m w", s=4, w=2)
             for s in range(2):
-                nc.scalar.copy(
-                    out=words[:, 2 * (pair % 2) + s, :, :, :],
-                    in_=ut_banks[2 * pair + s][:].rearrange("p (g w m) -> p g m w", g=FG, w=2),
+                regroup(
+                    engines[s],
+                    words[:, 2 * (pair % 2) + s, :, :, :],
+                    ut_banks[2 * pair + s][:].rearrange("p (g w m) -> p g m w", g=FG, w=2),
                 )
 
-        def quantize_u(h, g):
-            cols = slice(HALF * h, HALF * (h + 1))
-            nc.vector.quantize_mx(
-                out=u_codes[:, g, cols].bitcast(FP8X4), scales=u_sc[:, g, cols], in_=u_grp[h][:, g, :]
-            )
+        def quantize_u(h, lo, hi):
+            cols = slice(HALF * h + lo, HALF * h + hi)
+            for g in range(FG):
+                nc.vector.quantize_mx(
+                    out=u_codes[:, g, cols].bitcast(FP8X4),
+                    scales=u_sc[:, g, cols],
+                    in_=u_grp[h][:, g, PACK * lo : PACK * hi],
+                )
 
         def group_r(c, g):
-            grp = stage.tile([P, PACK * PASS], BF16, name="r_grp%d%d" % (c, g), tag="r_grp", bufs=5, align_bytes=64)
+            tag, bufs = ("u_grp", 2) if (c, g) == (2, 1) else ("r_grp", 4)
+            grp = stage.tile([P, PACK * PASS], BF16, name="r_grp%d%d" % (c, g), tag=tag, bufs=bufs, align_bytes=64)
             r_grp[c, g] = grp
             dst = grp[:].rearrange("p (t n j) -> p t n j", t=PACK, j=PACK)
             src = r_raw[:, c, g, :, :].rearrange("p j (n t) -> p t n j", t=PACK)
@@ -203,11 +209,12 @@ def tile_coulomb_response_mixing_h2_kernel(
                 for a in range(width // P):
                     nc.tensor.transpose(bank[:, a * P : (a + 1) * P], words[:, m0 // P + a, w::2], ident_f[:])
 
-        def scale_prev(i):
+        def scale_prev(i, slots):
             c, width = i // 2, HALF
-            tile = stage.tile([P, PACK, width], F32, name="kept%d" % i, tag="kept", bufs=2, align_bytes=64)
-            kept[i] = tile
-            for t in range(PACK):
+            if 0 in slots:
+                kept[i] = stage.tile([P, PACK, width], F32, name="kept%d" % i, tag="kept", bufs=2, align_bytes=64)
+            tile = kept[i]
+            for t in slots:
                 pairs = prev_banks[i, t // 2][:, 0:width].bitcast(BF16).rearrange("p (m e) -> p e m", e=2)
                 nc.scalar.activation(
                     out=tile[:, t, :],
@@ -216,11 +223,11 @@ def tile_coulomb_response_mixing_h2_kernel(
                     scale=rest_f[:, PACK * c + t : PACK * c + t + 1],
                 )
 
-        def second_product(i):
+        def second_product(i, slots):
             c, m0, width = UNITS[i]
             cols = slice(m0, m0 + width)
             per_bank = HALF // width
-            for t in range(PACK):
+            for t in slots:
                 if t % per_bank == 0:
                     bank = next_bank()
                 lo = (t % per_bank) * width
@@ -263,7 +270,7 @@ def tile_coulomb_response_mixing_h2_kernel(
 
         def store_y(i, a, engine):
             c, m0, width = UNITS[i]
-            rows = stage.tile([P, PASS], F32, name="y_rows%d%d" % (i, a), tag="y_rows", bufs=8, align_bytes=64)
+            rows = stage.tile([P, PASS], F32, name="y_rows%d%d" % (i, a), tag="y_rows", bufs=6, align_bytes=64)
             regroup(
                 engine,
                 rows[:].rearrange("m (p t) -> m p t", t=PACK),
@@ -276,12 +283,15 @@ def tile_coulomb_response_mixing_h2_kernel(
             width = UNITS[i][2]
             grp = stage.tile([P, width * PACK], BF16, name="y_grp%d" % i, tag="y_grp", bufs=2, align_bytes=64)
             y_grp[i] = grp
-            dst = grp[:].rearrange("p (m t) -> p m t", t=PACK)
-            src = y_t[i][:].rearrange("p t m -> p m t")
-            pieces = 2 if Y_ENGINE[i] == "G" else 1
-            step = width // pieces
-            for k in range(pieces):
-                regroup(Y_ENGINE[i], dst[:, k * step : (k + 1) * step], src[:, k * step : (k + 1) * step])
+            if Y_ENGINE[i] == "G":
+                dst = grp[:].rearrange("p (k m t) -> p k m t", k=2, t=PACK)
+                src = y_t[i][:].rearrange("p t (k m) -> p k m t", k=2)
+                for k in range(2):
+                    regroup("G", dst[:, k], src[:, k])
+            else:
+                dst = grp[:].rearrange("p (b i t) -> p b t i", i=4, t=PACK)
+                src = y_t[i][:].rearrange("p t (b i) -> p b t i", i=4)
+                regroup(Y_ENGINE[i], dst, src)
 
         def quantize_y(i):
             c, m0, width = UNITS[i]
@@ -294,10 +304,10 @@ def tile_coulomb_response_mixing_h2_kernel(
             dst = out_1[c].rearrange("p m t -> p (m t)").bitcast(I32)
             nc.sync.dma_start(out=dst[:, cols], in_=y_codes[:, c, cols].bitcast(I32))
             if m0 + width == M:
-                for q in range(4):
+                for j in range(4):
                     nc.sync.dma_start(
-                        out=out_2[c, 4 * q : 4 * q + 4, :].bitcast(I32),
-                        in_=y_sc[32 * q : 32 * q + 4, c, :].bitcast(I32),
+                        out=out_2[c].rearrange("(q j) m -> j q m", j=4)[j].bitcast(I32),
+                        in_=y_sc[j:P:32, c, :].bitcast(I32),
                     )
 
         nc.gpsimd.memset(c_sc[:].bitcast(I32), 0)
@@ -307,18 +317,17 @@ def tile_coulomb_response_mixing_h2_kernel(
         make_identity(nc, ident_f[:])
         load_c(0, 1)
         load_x(0, 0, 1)
-        for q in range(4):
-            load_scales(nc.sync, x_sc, x_scales, q)
-        for q in range(4):
-            load_scales(nc.sync, c_sc, c_scales, q)
+        load_scales(x_sc[:, 0], x_scales, 0, HALF)
+        load_scales(c_sc[:], c_scales, 0, F)
         nc.sync.dma_start(out=v_cols[:], in_=v.rearrange("(g p t) -> p g t", g=FG, t=PACK))
         nc.sync.dma_start(out=field_rows[0:MT, :], in_=field.rearrange("(a p) -> a p", p=P))
         load_c(1, KG)
         load_x(0, 1, KG)
         load_r(0, 0)
         load_r(0, 1)
-        load_x(1, 0, KG)
         load_r(1, 0)
+        load_scales(x_sc[:, 1], x_scales, HALF, M)
+        load_x(1, 0, KG)
         load_r(1, 1)
         nc.sync.dma_start(out=eta_b[:], in_=eta.rearrange("(c p t) -> p c t", c=NG, t=PACK))
         load_r(2, 0)
@@ -348,10 +357,11 @@ def tile_coulomb_response_mixing_h2_kernel(
             in_=v_bank[:].rearrange("m (a e p) -> m a p e", p=P, e=2),
         )
 
+        group_r(0, 0)
+        group_r(1, 0)
         add_external(0)
         add_external(1)
         first_product(1)
-        group_r(0, 0)
         group_r(0, 1)
         turn_u(0)
         add_external(2)
@@ -359,7 +369,7 @@ def tile_coulomb_response_mixing_h2_kernel(
         copy_u(0)
         first_product(2)
         quantize_r(0, 0)
-        group_r(1, 0)
+        quantize_r(1, 0)
         group_r(1, 1)
         turn_u(1)
         copy_u(1)
@@ -367,49 +377,48 @@ def tile_coulomb_response_mixing_h2_kernel(
         add_external(5)
         first_product(3)
         quantize_r(0, 1)
+        quantize_r(1, 1)
         group_r(2, 0)
-        group_r(2, 1)
         eta_flat = eta_b[:].rearrange("p c t -> p (c t)")
         nc.scalar.copy(out=eta_f[:], in_=eta_flat)
         nc.scalar.activation(out=rest_f[:], in_=eta_flat, func=ACT.Copy, scale=-1.0, bias=1.0)
         turn_u(2)
+        quantize_u(0, 0, HALF)
         add_external(6)
         add_external(7)
         copy_u(2)
+        group_r(2, 1)
+        quantize_u(1, 0, 2 * P)
         turn_prev(0)
-        scale_prev(0)
-        turn_u(3)
-        copy_u(3)
-        quantize_u(0, 0)
-        quantize_u(0, 1)
-        quantize_r(1, 0)
-        quantize_r(1, 1)
-        second_product(0)
-        for i in range(5):
-            mix(i, (0, 1, 2))
+        scale_prev(0, range(PACK))
+        for i in range(6):
+            second_product(i, (0, 1) if i < 5 else range(PACK))
+            mix(i, (0, 1))
             if i == 0:
-                quantize_u(1, 0)
-            if i in (1, 2):
-                quantize_r(2, i - 1)
-            mix(i, (3,))
+                turn_u(3)
+                copy_u(3)
+            else:
+                turn_y(i - 1)
+                store_y(i - 1, 0, "V")
+            if i < 5:
+                second_product(i, (2, 3))
+            else:
+                second_product(6, range(PACK))
+            if i in (2, 3):
+                quantize_r(2, i - 2)
             if i == 0:
-                quantize_u(1, 1)
+                quantize_u(1, 2 * P, HALF)
+            mix(i, (2, 3))
             if i > 0:
                 quantize_y(i - 1)
+                for a in range(1, 4):
+                    store_y(i - 1, a, "S")
                 store_planes(i - 1)
-            turn_prev(i + 1)
-            turn_y(i)
             group_y(i)
-            scale_prev(i + 1)
-            second_product(i + 1)
-            for a in range(4):
-                store_y(i, a, "V" if a == 0 else "S")
-        second_product(6)
-        mix(5, range(PACK))
-        quantize_y(4)
-        store_planes(4)
+            if i < 5:
+                turn_prev(i + 1)
+                scale_prev(i + 1, range(PACK))
         turn_y(5)
-        group_y(5)
         mix(6, range(PACK))
         turn_y(6)
         store_y(5, 0, "S")

from contextlib import ExitStack

import concourse.mybir as mybir
from concourse.masks import make_identity

M, K, F, N = 1024, 1536, 1024, 1536
FLOPS = 2 * M * K * F + 2 * M * F * N

F32 = mybir.dt.float32
BF16 = mybir.dt.bfloat16
I32 = mybir.dt.int32
U32 = mybir.dt.uint32
U8 = mybir.dt.uint8
FP8X4 = mybir.dt.float8_e4m3fn_x4
FP4X4 = mybir.dt.float4_e2m1fn_x4
ALU = mybir.AluOpType
ACT = mybir.ActivationFunctionType

P = 128
PACK = 4
PASS = P * PACK
KG = K // PASS
FG = F // PASS
NG = N // PASS
HALF = 512
MT = M // P
PAIRS = MT // 2
UNITS = [(0, 0, 512), (0, 512, 512), (1, 0, 512), (1, 512, 512), (2, 0, 512), (2, 512, 256), (2, 768, 256)]
R_ENGINE = {(0, 0): "S", (0, 1): "G", (1, 0): "S", (1, 1): "G", (2, 0): "S", (2, 1): "G"}
Y_ENGINE = ["G", "G", "G", "G", "G", "G", "V"]
BANKS = 8


def tile_coulomb_response_mixing_h2_kernel(
    tc, x_words, x_scales, c_words, c_scales, v, field, r, prev, eta, out_0, out_1, out_2
):
    nc = tc.nc
    with ExitStack() as ctx:
        keep = ctx.enter_context(tc.tile_pool(name="keep", bufs=1))
        stage = ctx.enter_context(tc.tile_pool(name="stage", bufs=3))
        psum = ctx.enter_context(tc.psum_pool(name="psum", bufs=1))
        ctx.enter_context(tc.manual_schedule())

        banks_taken = []

        def next_bank(dtype=F32):
            i = len(banks_taken)
            banks_taken.append(i)
            width = 512 if dtype == F32 else 1024
            return psum.tile([P, width], dtype, name="bank%d" % i, tag="bank%d" % (i % BANKS))

        x_codes = keep.tile([P, 2, KG, HALF], U32, name="x_codes", align_bytes=64)
        x_sc = keep.tile([P, 2, KG, HALF], U8, name="x_sc", align_bytes=64)
        c_codes = keep.tile([P, KG, 2 * F], U8, name="c_codes", align_bytes=64)
        c_sc = keep.tile([P, KG, F], U8, name="c_sc", align_bytes=64)
        r_raw = keep.tile([P, NG, FG, PACK, PASS], BF16, name="r_raw", align_bytes=64)
        r_codes = keep.tile([P, NG, FG, PASS], U32, name="r_codes", align_bytes=64)
        r_sc = keep.tile([P, NG, FG, PASS], U8, name="r_sc", align_bytes=64)
        prev_sb = keep.tile([P, NG, MT, PASS], BF16, name="prev_sb", align_bytes=64)
        u_codes = keep.tile([P, FG, M], U32, name="u_codes", align_bytes=64)
        u_sc = keep.tile([P, FG, M], U8, name="u_sc", align_bytes=64)
        y_codes = keep.tile([P, NG, M], U32, name="y_codes", align_bytes=64)
        y_sc = keep.tile([P, NG, M], U8, name="y_sc", align_bytes=64)
        ident_f = keep.tile([P, P], F32, name="ident_f", align_bytes=64)
        ident_b = keep.tile([P, P], BF16, name="ident_b", align_bytes=64)
        v_cols = keep.tile([P, FG, PACK], BF16, name="v_cols", align_bytes=64)
        v_rows = keep.tile([P, F], BF16, name="v_rows", align_bytes=64)
        field_rows = keep.tile([P, P], BF16, name="field_rows", align_bytes=64)
        field_cols = keep.tile([P, MT], F32, name="field_cols", align_bytes=64)
        eta_b = keep.tile([P, NG, PACK], BF16, name="eta_b", align_bytes=64)
        eta_f = keep.tile([P, NG * PACK], F32, name="eta_f", align_bytes=64)
        rest_f = keep.tile([P, NG * PACK], F32, name="rest_f", align_bytes=64)

        x_view = x_words.rearrange("g p m t -> p g (m t)").bitcast(I32)
        c_view = c_words.rearrange("g p b -> p g b").bitcast(I32)

        def load_x(h, g0, g1):
            nc.sync.dma_start(
                out=x_codes[:, h, g0:g1, :].bitcast(I32), in_=x_view[:, g0:g1, h * HALF : (h + 1) * HALF]
            )

        def load_c(g0, g1):
            nc.sync.dma_start(out=c_codes[:, g0:g1, :].bitcast(I32), in_=c_view[:, g0:g1, :])

        def load_scales(tile, src, lo, hi):
            for j in range(4):
                nc.sync.dma_start(
                    out=tile[j:P:32].bitcast(I32),
                    in_=src.rearrange("g (q j) n -> j q g n", j=4)[j, :, :, lo:hi].bitcast(I32),
                )

        def load_r(c, g):
            rows = r[g * PASS : (g + 1) * PASS, c * PASS : (c + 1) * PASS]
            nc.sync.dma_start(out=r_raw[:, c, g, :, :], in_=rows.rearrange("(p j) n -> p j n", j=PACK))

        def load_prev(c, h):
            rows = prev[h * HALF : (h + 1) * HALF, c * PASS : (c + 1) * PASS]
            nc.sync.dma_start(out=prev_sb[:, c, 4 * h : 4 * h + 4, :], in_=rows.rearrange("(a p) n -> p a n", p=P))

        def regroup(engine, dst, src):
            if engine == "S":
                nc.scalar.copy(out=dst, in_=src)
            elif engine == "V":
                nc.vector.tensor_copy(out=dst, in_=src)
            else:
                nc.gpsimd.tensor_scalar(out=dst, in0=src, scalar1=1.0, scalar2=1.0, op0=ALU.mult, op1=ALU.mult)

        u_banks = {}
        u_rows = {}
        ut_banks = {}
        u_grp = {}
        r_grp = {}

        def first_pass(mt, g, kg):
            if kg == 0:
                u_banks[mt, g] = next_bank()
            col = (mt % 4) * P
            nc.tensor.matmul_mx(
                out=u_banks[mt, g][:],
                lhsT=x_codes[:, mt // 4, kg, col : col + P].bitcast(FP8X4),
                lhsT_scale=x_sc[:, mt // 4, kg, col : col + P],
                rhs=c_codes[:, kg, 2 * g * PASS : 2 * (g + 1) * PASS].bitcast(FP4X4),
                rhs_scale=c_sc[:, kg, g * PASS : (g + 1) * PASS],
                start=(kg == 0),
                stop=(kg == KG - 1),
            )

        def first_product(pair):
            for mt in (2 * pair, 2 * pair + 1):
                for g in range(FG):
                    for kg in range(KG):
                        first_pass(mt, g, kg)

        def add_external(mt):
            rows = stage.tile([P, FG, 2, P, 2], BF16, name="u_rows%d" % mt, tag="u_rows", bufs=4, align_bytes=64)
            u_rows[mt] = rows
            for g in range(FG):
                sums = u_banks[mt, g][:].rearrange("m (p w e) -> m w p e", w=2, e=2)
                for w in range(2):
                    lo = (2 * g + w) * 2 * P
                    nc.vector.scalar_tensor_tensor(
                        out=rows[:, g, w, :, :],
                        in0=v_rows[:, lo : lo + 2 * P].rearrange("m (p e) -> m p e", e=2),
                        scalar=field_cols[:, mt : mt + 1],
                        in1=sums[:, w, :, :],
                        op0=ALU.mult,
                        op1=ALU.add,
                    )

        def turn_u(pair):
            for mt in (2 * pair, 2 * pair + 1):
                bank = next_bank()
                ut_banks[mt] = bank
                words = u_rows[mt][:].rearrange("m g w p e -> m (g w p e)").bitcast(F32)
                for a in range(2 * FG):
                    nc.tensor.transpose(bank[:, a * P : (a + 1) * P], words[:, a * P : (a + 1) * P], ident_f[:])

        def copy_u(pair, engines="SS"):
            h = pair // 2
            if pair % 2 == 0:
                u_grp[h] = stage.tile([P, FG, HALF * PACK], BF16, name="u_grp%d" % h, tag="u_grp", bufs=2, align_bytes=64)
            words = u_grp[h][:].bitcast(F32).rearrange("p g (s m w) -> p s g m w", s=4, w=2)
            for s in range(2):
                regroup(
                    engines[s],
                    words[:, 2 * (pair % 2) + s, :, :, :],
                    ut_banks[2 * pair + s][:].rearrange("p (g w m) -> p g m w", g=FG, w=2),
                )

        def quantize_u(h, lo, hi):
            cols = slice(HALF * h + lo, HALF * h + hi)
            for g in range(FG):
                nc.vector.quantize_mx(
                    out=u_codes[:, g, cols].bitcast(FP8X4),
                    scales=u_sc[:, g, cols],
                    in_=u_grp[h][:, g, PACK * lo : PACK * hi],
                )

        def group_r(c, g):
            tag, bufs = ("u_grp", 2) if (c, g) == (2, 1) else ("r_grp", 4)
            grp = stage.tile([P, PACK * PASS], BF16, name="r_grp%d%d" % (c, g), tag=tag, bufs=bufs, align_bytes=64)
            r_grp[c, g] = grp
            dst = grp[:].rearrange("p (t n j) -> p t n j", t=PACK, j=PACK)
            src = r_raw[:, c, g, :, :].rearrange("p j (n t) -> p t n j", t=PACK)
            if R_ENGINE[c, g] == "G":
                for t in range(PACK):
                    regroup("G", dst[:, t], src[:, t])
            else:
                regroup(R_ENGINE[c, g], dst, src)

        def quantize_r(c, g):
            nc.vector.quantize_mx(
                out=r_codes[:, c, g, :].bitcast(FP8X4), scales=r_sc[:, c, g, :], in_=r_grp[c, g][:]
            )

        prev_banks = {}
        kept = {}
        z_banks = {}
        y_t = {}
        y_banks = {}
        y_grp = {}

        def turn_prev(i):
            c, m0, width = i // 2, (i % 2) * HALF, HALF
            words = prev_sb[:, c, :, :].bitcast(F32)
            for w in range(2):
                bank = next_bank()
                prev_banks[i, w] = bank
                for a in range(width // P):
                    nc.tensor.transpose(bank[:, a * P : (a + 1) * P], words[:, m0 // P + a, w::2], ident_f[:])

        def scale_prev(i, slots):
            c, width = i // 2, HALF
            if 0 in slots:
                kept[i] = stage.tile([P, PACK, width], F32, name="kept%d" % i, tag="kept", bufs=2, align_bytes=64)
            tile = kept[i]
            for t in slots:
                pairs = prev_banks[i, t // 2][:, 0:width].bitcast(BF16).rearrange("p (m e) -> p e m", e=2)
                nc.scalar.activation(
                    out=tile[:, t, :],
                    in_=pairs[:, t % 2, :],
                    func=ACT.Copy,
                    scale=rest_f[:, PACK * c + t : PACK * c + t + 1],
                )

        def second_product(i, slots):
            c, m0, width = UNITS[i]
            cols = slice(m0, m0 + width)
            per_bank = HALF // width
            for t in slots:
                if t % per_bank == 0:
                    bank = next_bank()
                lo = (t % per_bank) * width
                z_banks[i, t] = bank[:, lo : lo + width]
                for g in range(FG):
                    nc.tensor.matmul_mx(
                        out=z_banks[i, t],
                        lhsT=r_codes[:, c, g, t * P : (t + 1) * P].bitcast(FP8X4),
                        lhsT_scale=r_sc[:, c, g, t * P : (t + 1) * P],
                        rhs=u_codes[:, g, cols].bitcast(FP8X4),
                        rhs_scale=u_sc[:, g, cols],
                        start=(g == 0),
                        stop=(g == FG - 1),
                    )

        def mix(i, slots):
            c, m0, width = UNITS[i]
            if 0 in slots:
                y_t[i] = stage.tile([P, PACK, width], F32, name="y_t%d" % i, tag="y_t", bufs=3, align_bytes=64)
            tile = y_t[i]
            for t in slots:
                nc.vector.scalar_tensor_tensor(
                    out=tile[:, t, :],
                    in0=z_banks[i, t],
                    scalar=eta_f[:, PACK * c + t : PACK * c + t + 1],
                    in1=kept[2 * c + m0 // HALF][:, t, m0 % HALF : m0 % HALF + width],
                    op0=ALU.mult,
                    op1=ALU.add,
                )

        def turn_y(i):
            tiles = range(UNITS[i][2] // P)
            for a in tiles:
                y_banks[i, a] = next_bank()
            for t in range(PACK):
                for a in tiles:
                    nc.tensor.transpose(
                        y_banks[i, a][:, t * P : (t + 1) * P], y_t[i][:, t, a * P : (a + 1) * P], ident_f[:]
                    )

        def store_y(i, a, engine):
            c, m0, width = UNITS[i]
            rows = stage.tile([P, PASS], F32, name="y_rows%d%d" % (i, a), tag="y_rows", bufs=6, align_bytes=64)
            regroup(
                engine,
                rows[:].rearrange("m (p t) -> m p t", t=PACK),
                y_banks[i, a][:].rearrange("m (t p) -> m p t", t=PACK),
            )
            lo = m0 + a * P
            nc.sync.dma_start(out=out_0[lo : lo + P, c * PASS : (c + 1) * PASS], in_=rows[:])

        def group_y(i):
            width = UNITS[i][2]
            grp = stage.tile([P, width * PACK], BF16, name="y_grp%d" % i, tag="y_grp", bufs=2, align_bytes=64)
            y_grp[i] = grp
            if Y_ENGINE[i] == "G":
                dst = grp[:].rearrange("p (k m t) -> p k m t", k=2, t=PACK)
                src = y_t[i][:].rearrange("p t (k m) -> p k m t", k=2)
                for k in range(2):
                    regroup("G", dst[:, k], src[:, k])
            else:
                dst = grp[:].rearrange("p (b i t) -> p b t i", i=4, t=PACK)
                src = y_t[i][:].rearrange("p t (b i) -> p b t i", i=4)
                regroup(Y_ENGINE[i], dst, src)

        def quantize_y(i):
            c, m0, width = UNITS[i]
            cols = slice(m0, m0 + width)
            nc.vector.quantize_mx(out=y_codes[:, c, cols].bitcast(FP8X4), scales=y_sc[:, c, cols], in_=y_grp[i][:])

        def store_planes(i):
            c, m0, width = UNITS[i]
            cols = slice(m0, m0 + width)
            dst = out_1[c].rearrange("p m t -> p (m t)").bitcast(I32)
            nc.sync.dma_start(out=dst[:, cols], in_=y_codes[:, c, cols].bitcast(I32))
            if m0 + width == M:
                for j in range(4):
                    nc.sync.dma_start(
                        out=out_2[c].rearrange("(q j) m -> j q m", j=4)[j].bitcast(I32),
                        in_=y_sc[j:P:32, c, :].bitcast(I32),
                    )

        nc.gpsimd.memset(c_sc[:].bitcast(I32), 0)
        nc.vector.memset(x_sc[:].bitcast(I32), 0)
        nc.vector.memset(field_rows[:], 0.0)
        make_identity(nc, ident_b[:])
        make_identity(nc, ident_f[:])
        load_c(0, 1)
        load_x(0, 0, 1)
        load_scales(x_sc[:, 0], x_scales, 0, HALF)
        load_scales(c_sc[:], c_scales, 0, F)
        nc.sync.dma_start(out=v_cols[:], in_=v.rearrange("(g p t) -> p g t", g=FG, t=PACK))
        nc.sync.dma_start(out=field_rows[0:MT, :], in_=field.rearrange("(a p) -> a p", p=P))
        load_c(1, KG)
        load_x(0, 1, KG)
        load_r(0, 0)
        load_r(0, 1)
        load_r(1, 0)
        load_scales(x_sc[:, 1], x_scales, HALF, M)
        load_x(1, 0, KG)
        load_r(1, 1)
        nc.sync.dma_start(out=eta_b[:], in_=eta.rearrange("(c p t) -> p c t", c=NG, t=PACK))
        load_r(2, 0)
        load_r(2, 1)
        load_prev(0, 0)
        load_prev(0, 1)
        for c in range(1, NG):
            load_prev(c, 0)
            load_prev(c, 1)

        for mt in range(2):
            for g in range(FG):
                first_pass(mt, g, 0)
        v_bank = next_bank(BF16)
        for a in range(FG * PACK):
            col = v_cols[:].rearrange("p g t -> p (g t)")[:, a : a + 1]
            nc.tensor.transpose(v_bank[:, a * P : (a + 1) * P], col.to_broadcast([P, P]), ident_b[:])
        field_bank = next_bank(BF16)
        nc.tensor.transpose(field_bank[:, 0:P], field_rows[:], ident_b[:])
        for kg in range(1, KG):
            for mt in range(2):
                for g in range(FG):
                    first_pass(mt, g, kg)
        nc.scalar.activation(out=field_cols[:], in_=field_bank[:, 0:MT], func=ACT.Copy)
        nc.vector.tensor_copy(
            out=v_rows[:].rearrange("m (a p e) -> m a p e", p=P, e=2),
            in_=v_bank[:].rearrange("m (a e p) -> m a p e", p=P, e=2),
        )

        group_r(0, 0)
        group_r(1, 0)
        add_external(0)
        add_external(1)
        first_product(1)
        group_r(0, 1)
        turn_u(0)
        add_external(2)
        add_external(3)
        copy_u(0)
        first_product(2)
        quantize_r(0, 0)
        quantize_r(1, 0)
        group_r(1, 1)
        turn_u(1)
        copy_u(1)
        add_external(4)
        add_external(5)
        first_product(3)
        quantize_r(0, 1)
        quantize_r(1, 1)
        group_r(2, 0)
        eta_flat = eta_b[:].rearrange("p c t -> p (c t)")
        nc.scalar.copy(out=eta_f[:], in_=eta_flat)
        nc.scalar.activation(out=rest_f[:], in_=eta_flat, func=ACT.Copy, scale=-1.0, bias=1.0)
        turn_u(2)
        quantize_u(0, 0, HALF)
        add_external(6)
        add_external(7)
        copy_u(2)
        group_r(2, 1)
        quantize_u(1, 0, 2 * P)
        turn_prev(0)
        scale_prev(0, range(PACK))
        for i in range(6):
            second_product(i, (0, 1) if i < 5 else range(PACK))
            mix(i, (0, 1))
            if i == 0:
                turn_u(3)
                copy_u(3)
            else:
                turn_y(i - 1)
                store_y(i - 1, 0, "V")
            if i < 5:
                second_product(i, (2, 3))
            else:
                second_product(6, range(PACK))
            if i in (2, 3):
                quantize_r(2, i - 2)
            if i == 0:
                quantize_u(1, 2 * P, HALF)
            mix(i, (2, 3))
            if i > 0:
                quantize_y(i - 1)
                for a in range(1, 4):
                    store_y(i - 1, a, "S")
                store_planes(i - 1)
            group_y(i)
            if i < 5:
                turn_prev(i + 1)
                scale_prev(i + 1, range(PACK))
        turn_y(5)
        mix(6, range(PACK))
        turn_y(6)
        store_y(5, 0, "S")
        store_y(5, 1, "S")
        quantize_y(5)
        store_planes(5)
        group_y(6)
        store_y(6, 0, "S")
        store_y(6, 1, "S")
        quantize_y(6)
        store_planes(6)
